import numpy as np
import ml_dtypes


def mxq(x, axis, fmt="e4m3"):
    dtype, down = {"e4m3": (ml_dtypes.float8_e4m3fn, 7), "e5m2": (ml_dtypes.float8_e5m2, 14)}[fmt]
    v = np.moveaxis(np.asarray(x, np.float32).astype(ml_dtypes.bfloat16).astype(np.float64), axis, -1)
    blocks = v.reshape(v.shape[:-1] + (-1, 32))
    amax = np.abs(blocks).max(-1, keepdims=True)
    byte = np.maximum(np.where(amax > 0, np.frexp(amax)[1] - 1 + 127, 0) - down, 1)
    scale = np.exp2(byte - 127.0)
    codes = (blocks / scale).astype(np.float32).astype(dtype).astype(np.float64)
    return np.moveaxis((codes * scale).reshape(v.shape), -1, axis)


WIDE = False


def mx_kscale(k):
    if not WIDE:
        return np.ones(k)
    levels = np.array([10, -10, 5, -5, 0])
    if k % 512:
        return np.exp2(np.random.permutation(np.resize(levels, k // 32))).repeat(32)
    a = np.empty((k // 512, 16))
    for p in range(k // 512):
        a[p, :8] = np.random.permutation(np.resize(levels, 8))
        for g in range(8):
            far = levels[np.abs(levels - a[p, g]) >= 10]
            a[p, g + 8] = far[np.random.randint(len(far))]
    return np.exp2(a.ravel()).repeat(32)


def f64(x):
    return np.asarray(x).astype(np.float64)


def striped(idx):
    return np.tile(idx.reshape(-1, 16).T, (8, 1)).astype(np.uint16)


def unstriped(offs):
    return offs[:16].T.reshape(-1).astype(np.int64)


def striped8(idx):
    return np.concatenate([x.reshape(-1, 16).T for x in idx]).astype(np.uint16)


def runs(offs, k):
    lists = np.stack([offs[16 * r : 16 * r + 16].T.reshape(-1) for r in range(8)]).astype(np.int64)
    return lists[np.arange(k) % 512 // 64]


def pack_weight(w):
    k, n = w.shape
    w = f64(np.asarray(w, np.float32).astype(ml_dtypes.bfloat16)).reshape(k // 32, 32, n)
    amax = np.abs(w).max(1)
    byte = np.clip(np.where(amax > 0, np.frexp(amax)[1] - 1 + 127 - 7, 1), 1, 254)
    scaled = (w * np.exp2(127.0 - byte)[:, None, :]).reshape(k, n).astype(np.float32)
    words = np.ascontiguousarray(scaled.reshape(k // 512, 128, 4, n).transpose(0, 1, 3, 2)).astype(ml_dtypes.float8_e4m3fn).view(np.uint8)
    return words, np.ascontiguousarray(byte.astype(np.uint8).reshape(k // 512, 16, n))


def unpack_weight(words, scales):
    g, p, n, _ = words.shape
    vals = np.ascontiguousarray(words).view(ml_dtypes.float8_e4m3fn).astype(np.float64) * np.repeat(np.exp2(scales.astype(np.float64) - 127.0), 8, axis=1)[..., None]
    return vals.transpose(0, 1, 3, 2).reshape(g * 512, n)


E2M1 = np.array([0.0, 0.5, 1.0, 1.5, 2.0, 3.0, 4.0, 6.0, -0.0, -0.5, -1.0, -1.5, -2.0, -3.0, -4.0, -6.0])


def pack_fp4(w):
    k, n = w.shape
    w = f64(np.asarray(w, np.float32).astype(ml_dtypes.bfloat16)).reshape(k // 32, 32, n)
    amax = np.abs(w).max(1)
    mant, ex = np.frexp(amax / 6.0)
    byte = np.clip(np.where(amax > 0, np.where(mant > 0.5, ex, ex - 1) + 127, 1), 1, 254)
    scaled = (w * np.exp2(127.0 - byte)[:, None, :]).reshape(k, n).astype(np.float32)
    c = np.ascontiguousarray(scaled.reshape(k // 512, 128, 4, n).transpose(0, 1, 3, 2)).astype(ml_dtypes.float4_e2m1fn).view(np.uint8) & 0xF
    words = (c[..., 0::2] | (c[..., 1::2] << 4)).reshape(k // 512, 128, 2 * n)
    return np.ascontiguousarray(words), np.ascontiguousarray(byte.astype(np.uint8).reshape(k // 512, 16, n))


def unpack_fp4(words, scales):
    g, _, n = scales.shape
    words = np.ascontiguousarray(words).reshape(g, 128, n, 2)
    nib = np.empty((g, 128, n, 4), np.uint8)
    nib[..., 0::2] = words & 0xF
    nib[..., 1::2] = words >> 4
    vals = E2M1[nib] * np.repeat(np.exp2(scales.astype(np.float64) - 127.0), 8, axis=1)[..., None]
    return vals.transpose(0, 1, 3, 2).reshape(g * 512, n)


def relu(v):
    return np.maximum(v, 0.0)

def planes(y):
    n, m = y.shape
    v = y.astype(np.float32).astype(ml_dtypes.bfloat16).astype(np.float64).reshape(n // 32, 32, m)
    top = np.abs(v).max(1)
    byte = np.clip(np.where(top > 0, np.frexp(top)[1] - 1 + 127 - 7, 1), 1, 254)
    codes = (v * np.exp2(127.0 - byte)[:, None, :]).reshape(n, m).astype(np.float32).astype(ml_dtypes.float8_e4m3fn).view(np.uint8)
    words = codes.reshape(n // 512, 128, 4, m).transpose(0, 1, 3, 2)
    return np.ascontiguousarray(words), np.ascontiguousarray(byte.astype(np.uint8).reshape(n // 512, 16, m))


K, T, S, N, H, J, G, U = 512, 1024, 512, 512, 512, 512, 2048, 1024


def setup_inputs():
    n = np.random.standard_normal
    s = mx_kscale(K)[:, None]
    u = mx_kscale(S)
    packed_xT = pack_weight(n((K, T)) * s)
    packed_w1 = pack_fp4(n((K, H)) / np.sqrt(K) / s)
    packed_dT = pack_weight(n((K, G)) / s)
    packed_w2 = pack_fp4(n((H, N)) / np.sqrt(H) / u[:, None])
    return {
        "x_words": packed_xT[0],
        "x_scales": packed_xT[1],
        "w1_words": packed_w1[0],
        "w1_scales": packed_w1[1],
        "tab": n((H, J)).astype(np.float32),
        "gs": (np.random.uniform(0.5, 1.5, (K, 1)) * s).astype(np.float32),
        "d_words": packed_dT[0],
        "d_scales": packed_dT[1],
        "res": (1.5 * n((N, U))).astype(np.float32),
        "gn": (np.random.uniform(0.5, 1.5, (H, 1)) * u[:, None]).astype(np.float32),
        "w2_words": packed_w2[0],
        "w2_scales": packed_w2[1],
        "offs": striped(np.random.permutation(T)[:S]),
        "n1": striped8(np.random.randint(0, J, (8, S))),
        "n2": striped8(np.random.randint(0, J, (8, S))),
        "n3": striped8(np.stack([np.random.permutation(S) for _ in range(8)])),
        "kidx": striped8(np.random.randint(0, G, (8, H))),
        "n4": striped8(np.stack([np.random.permutation(U)[:S] for _ in range(8)])),
        "n5": striped8(np.stack([np.random.permutation(S) for _ in range(8)])),
    }


def reference(x_words, x_scales, w1_words, w1_scales, tab, gs, d_words, d_scales, res, gn, w2_words, w2_scales, offs, n1, n2, n3, kidx, n4, n5):
    d_kidx = unpack_weight(d_words, d_scales)[np.arange(K)[:, None], runs(kidx, K)]
    xq = unpack_weight(x_words, x_scales)[:, unstriped(offs)]
    y = unpack_fp4(w1_words, w1_scales).T @ xq
    z = f64(gs) * ((y[np.arange(H)[:, None], runs(n3, H)]) * (f64(tab)[np.arange(H)[:, None], runs(n1, H)]) + f64(tab)[np.arange(H)[:, None], runs(n2, H)])
    s = 0.0625 * ((d_kidx.T @ mxq(z, 0, "e4m3")))
    nw = s - (relu(s[np.arange(H)[:, None], runs(n5, H)]))
    pg = np.zeros((H, U))
    pg[np.arange(H)[:, None], runs(n4, H)] = nw
    z2 = f64(gn) * pg
    out_0 = f64(res) + (unpack_fp4(w2_words, w2_scales).T @ mxq(z2, 0, "e4m3"))
    return (out_0,) + planes(out_0)

@@ -1,0 +1,254 @@
+from contextlib import ExitStack
+
+import concourse.mybir as mybir
+
+F32 = mybir.dt.float32
+BF16 = mybir.dt.bfloat16
+I32 = mybir.dt.int32
+U32 = mybir.dt.uint32
+U16 = mybir.dt.uint16
+U8 = mybir.dt.uint8
+FP8X4 = mybir.dt.float8_e4m3fn_x4
+FP4X4 = mybir.dt.float4_e2m1fn_x4
+ALU = mybir.AluOpType
+ACT = mybir.ActivationFunctionType
+
+P = 128
+PACK = 4
+S = 512
+HALF = 256
+U = 1024
+CH = 256
+FLOPS = 2 * 512 * 512 * (512 + 512 + 1024)
+
+
+def tile_picked_pqkkindapagez_none_po_kernel(
+    tc, x_words, x_scales, w1_words, w1_scales, tab, gs, d_words, d_scales, res, gn, w2_words, w2_scales,
+    offs, n1, n2, n3, kidx, n4, n5, out_0, out_1, out_2,
+):
+    nc = tc.nc
+    with ExitStack() as ctx:
+        keep = ctx.enter_context(tc.tile_pool(name="keep", bufs=1))
+        psum = ctx.enter_context(tc.psum_pool(name="psum", bufs=8))
+
+        def sb(name, shape, dtype):
+            return keep.tile(shape, dtype, name=name, align_bytes=64)
+
+        def load_list(name, src):
+            lst = keep.tile([P, S // 16], U16, name=name)
+            nc.sync.dma_start(lst[:], src)
+            return lst
+
+        def zeroed_bytes(name, width):
+            plane = sb(name, [P, width], U8)
+            nc.vector.memset(plane[:].bitcast(I32), 0)
+            return plane
+
+        def load_scale_rows(plane, src):
+            for q in range(4):
+                nc.sync.dma_start(plane[32 * q : 32 * q + 4, :].bitcast(I32), src[0, 4 * q : 4 * q + 4, :].bitcast(I32))
+
+        def deal_fp4(name, raw_words, raw_scales):
+            words = sb(name + "_w", [P, 2 * S], U8)
+            nc.vector.tensor_copy(
+                words[:].rearrange("p (t m b) -> p t m b", t=PACK, b=2),
+                raw_words[:].rearrange("p (m t b) -> p t m b", t=PACK, b=2),
+            )
+            scales = sb(name + "_s", [P, S], U8)
+            nc.vector.tensor_copy(
+                scales[:].rearrange("p (t m) -> p t m", t=PACK),
+                raw_scales[:].rearrange("p (m t) -> p t m", t=PACK),
+            )
+            return words, scales
+
+        def interleave(dst, src):
+            nc.scalar.copy(
+                dst[:].rearrange("p (c i) t -> p c t i", i=4),
+                src[:].rearrange("p t (c i) -> p c t i", i=4),
+            )
+
+        def half_of(lst, h):
+            return lst[:, 16 * h : 16 * (h + 1)]
+
+        xs_win = zeroed_bytes("xs_win", 1024)
+        w1s_raw = zeroed_bytes("w1s_raw", S)
+        ds_win = zeroed_bytes("ds_win", 2048)
+        w2s_raw = zeroed_bytes("w2s_raw", S)
+        d_sc = zeroed_bytes("d_sc", S)
+        page = [sb("page%d" % t, [P, U], F32) for t in range(PACK)]
+        for t in range(PACK):
+            nc.gpsimd.memset(page[t][:], 0.0)
+
+        tab_rows = tab.rearrange("(p t) j -> t p j", t=PACK)
+        tab_win = [sb("tab%d" % t, [P, S], F32) for t in range(PACK)]
+        l1 = load_list("l1", n1)
+        nc.sync.dma_start(tab_win[0][:], tab_rows[0])
+        nc.sync.dma_start(tab_win[1][:], tab_rows[1])
+        lx = load_list("lx", offs)
+        xw_win = sb("xw_win", [P, 1024], I32)
+        nc.sync.dma_start(xw_win[:], x_words[0].rearrange("p c r -> p (c r)").bitcast(I32))
+        w1w_raw = sb("w1w_raw", [P, 2 * S], U8)
+        nc.sync.dma_start(w1w_raw[:].bitcast(I32), w1_words[0].bitcast(I32))
+        load_scale_rows(xs_win, x_scales)
+        load_scale_rows(w1s_raw, w1_scales)
+        nc.sync.dma_start(tab_win[2][:], tab_rows[2])
+        nc.sync.dma_start(tab_win[3][:], tab_rows[3])
+        gs_sb = sb("gs_sb", [P, PACK], F32)
+        nc.sync.dma_start(gs_sb[:], gs.rearrange("(p t) o -> p (t o)", t=PACK))
+        lk = load_list("lk", kidx)
+        d_rows = d_scales[0].rearrange("(r e) c -> e r c", e=2)
+        for e in range(2):
+            nc.sync.dma_start(ds_win[e:P:16, :].bitcast(I32), d_rows[e].bitcast(I32))
+        l3 = load_list("l3", n3)
+        l2 = load_list("l2", n2)
+        dw_win = sb("dw_win", [P, 2048], I32)
+        nc.sync.dma_start(dw_win[:], d_words[0].rearrange("p c r -> p (c r)").bitcast(I32))
+        gn_sb = sb("gn_sb", [P, PACK], F32)
+        nc.sync.dma_start(gn_sb[:], gn.rearrange("(p t) o -> p (t o)", t=PACK))
+        l5 = load_list("l5", n5)
+        l4 = load_list("l4", n4)
+        w2w_raw = sb("w2w_raw", [P, 2 * S], U8)
+        nc.sync.dma_start(w2w_raw[:].bitcast(I32), w2_words[0].bitcast(I32))
+        load_scale_rows(w2s_raw, w2_scales)
+        res_rows = res.rearrange("(p t) w -> p t w", t=PACK)
+        res_sb = [sb("res%d" % c, [P, PACK, CH], F32) for c in range(U // CH)]
+        for c in range(U // CH):
+            nc.sync.dma_start(res_sb[c][:], res_rows[:, :, CH * c : CH * (c + 1)])
+
+        t1 = [sb("t1_%d" % t, [P, S], F32) for t in range(PACK)]
+
+        def fetch_t1(t):
+            for h in range(2):
+                nc.vector.tensor_copy(t1[t][:, HALF * h : HALF * (h + 1)], tab_win[t][:].indirect(half_of(l1, h)))
+
+        fetch_t1(0)
+        fetch_t1(1)
+        xw = sb("xw", [P, S], I32)
+        nc.vector.tensor_copy(xw[:].bitcast(U32), xw_win[:].bitcast(U32).indirect(lx[:]))
+        xs = sb("xs", [P, S], U8)
+        nc.vector.tensor_copy(xs[:], xs_win[:].indirect(lx[:]))
+        w1w, w1s = deal_fp4("w1", w1w_raw, w1s_raw)
+
+        y_win = [sb("y%d" % t, [P, S], F32) for t in range(PACK)]
+        tabg = [sb("tabg%d" % t, [P, S], F32) for t in range(PACK)]
+        for t in range(PACK):
+            acc = psum.tile([P, S], F32, name="bank")
+            nc.tensor.matmul_mx(
+                out=acc[:], lhsT=w1w[:, 2 * P * t : 2 * P * (t + 1)].bitcast(FP4X4), lhsT_scale=w1s[:, P * t : P * (t + 1)],
+                rhs=xw[:].bitcast(FP8X4), rhs_scale=xs[:], start=True, stop=True,
+            )
+            nc.scalar.activation(y_win[t][:], acc[:], ACT.Copy, scale=gs_sb[:, t : t + 1])
+            nc.scalar.activation(tabg[t][:], tab_win[t][:], ACT.Copy, scale=gs_sb[:, t : t + 1])
+        fetch_t1(2)
+        fetch_t1(3)
+
+        dsg = sb("dsg", [P, S], U8)
+        nc.vector.tensor_copy(dsg[:], ds_win[:].indirect(lk[:]))
+        dsd = sb("dsd", [P, S], U8)
+        nc.vector.tensor_copy(dsd[:].rearrange("p (t m) -> p t m", t=PACK), dsg[:].rearrange("p (m t) -> p t m", t=PACK))
+        for r in range(4):
+            nc.sync.dma_start(d_sc[r:P:32, :].bitcast(I32), dsd[16 * (r // 2) + r % 2 : P : 32, :].bitcast(I32))
+        dwg = sb("dwg", [P, S], I32)
+        nc.vector.tensor_copy(dwg[:].bitcast(U32), dw_win[:].bitcast(U32).indirect(lk[:]))
+        dw = sb("dw", [P, S], I32)
+        nc.vector.tensor_copy(dw[:].rearrange("p (t m) -> p t m", t=PACK), dwg[:].rearrange("p (m t) -> p t m", t=PACK))
+
+        gpos = sb("gpos", [P, PACK], F32)
+        nc.scalar.activation(gpos[:], gn_sb[:], ACT.Copy, scale=0.0625)
+        gneg = sb("gneg", [P, PACK], F32)
+        nc.scalar.activation(gneg[:], gn_sb[:], ACT.Copy, scale=-0.0625)
+
+        s_acc = [psum.tile([P, S], F32, name="bank") for t in range(PACK)]
+        for h in range(2):
+            cols = slice(HALF * h, HALF * (h + 1))
+            prod = sb("prod%d" % h, [P, PACK, HALF], F32)
+            z = sb("z%d" % h, [P, PACK, HALF], F32)
+            for t in range(PACK):
+                nc.vector.tensor_tensor(prod[:, t, :], y_win[t][:].indirect(half_of(l3, h)), t1[t][:, cols], ALU.mult)
+            for t in range(PACK):
+                nc.vector.tensor_tensor(z[:, t, :], tabg[t][:].indirect(half_of(l2, h)), prod[:, t, :], ALU.add)
+            zb = sb("zb%d" % h, [P, HALF, PACK], BF16)
+            interleave(zb, z)
+            if h == 1:
+                w2w, w2s = deal_fp4("w2", w2w_raw, w2s_raw)
+            zw = sb("zw%d" % h, [P, HALF], I32)
+            zs = sb("zs%d" % h, [P, HALF], U8)
+            nc.vector.quantize_mx(out=zw[:].bitcast(FP8X4), scales=zs[:], in_=zb[:].rearrange("p c t -> p (c t)"))
+            for t in range(PACK):
+                nc.tensor.matmul_mx(
+                    out=s_acc[t][:, cols], lhsT=dw[:, P * t : P * (t + 1)].bitcast(FP8X4), lhsT_scale=d_sc[:, P * t : P * (t + 1)],
+                    rhs=zw[:].bitcast(FP8X4), rhs_scale=zs[:], start=True, stop=True,
+                )
+
+        z2b = [sb("z2b%d" % c, [P, CH, PACK], BF16) for c in range(U // CH)]
+        for t in range(PACK):
+            neg = sb("neg%d" % t, [P, S], F32)
+            if t == 0:
+                nc.vector.tensor_scalar(neg[:], s_acc[t][:], 0.0, gneg[:, t : t + 1], ALU.max, ALU.mult)
+            else:
+                pos = sb("pos%d" % t, [P, S], F32)
+                nc.scalar.activation(pos[:], s_acc[t][:], ACT.Relu)
+                nc.scalar.activation(neg[:], pos[:], ACT.Copy, scale=gneg[:, t : t + 1])
+            own = sb("own%d" % t, [P, S], F32)
+            nc.scalar.activation(own[:], s_acc[t][:], ACT.Copy, scale=gpos[:, t : t + 1])
+            got = sb("got%d" % t, [P, S], F32)
+            for h in range(2):
+                nc.vector.tensor_copy(got[:, HALF * h : HALF * (h + 1)], neg[:].indirect(half_of(l5, h)))
+            nc.vector.tensor_tensor(page[t][:].indirect(l4[:]), own[:], got[:], ALU.add)
+        for t in range(PACK):
+            for c in range(U // CH):
+                src = page[t][:, CH * c : CH * (c + 1)]
+                if t == 2 and c == 0:
+                    nc.scalar.copy(z2b[c][:, :, 2:4], src.unsqueeze(2).to_broadcast([P, CH, 2]))
+                elif t == 3 and c == 0:
+                    nc.vector.tensor_copy(z2b[c][:, :, t], src)
+                else:
+                    nc.scalar.copy(z2b[c][:, :, t], src)
+
+        out_rows = out_0.rearrange("(p t) w -> p t w", t=PACK)
+        out_words = out_1[0].rearrange("p c r -> p (c r)").bitcast(I32)
+        o_sc = sb("o_sc", [P, U], U8)
+        outs = []
+
+        def finish(c):
+            ob = sb("ob%d" % c, [P, CH, PACK], BF16)
+            interleave(ob, outs[c])
+            ow = sb("ow%d" % c, [P, CH], I32)
+            nc.vector.quantize_mx(out=ow[:].bitcast(FP8X4), scales=o_sc[:, CH * c : CH * (c + 1)], in_=ob[:].rearrange("p c t -> p (c t)"))
+            nc.sync.dma_start(out_words[:, CH * c : CH * (c + 1)], ow[:])
+
+        accs = []
+
+        def product(c):
+            qw = sb("qw%d" % c, [P, CH], I32)
+            qs = sb("qs%d" % c, [P, CH], U8)
+            nc.vector.quantize_mx(out=qw[:].bitcast(FP8X4), scales=qs[:], in_=z2b[c][:].rearrange("p c t -> p (c t)"))
+            pair = []
+            for k in range(2):
+                acc = psum.tile([P, 2, CH], F32, name="bank")
+                for e in range(2):
+                    t = 2 * k + e
+                    nc.tensor.matmul_mx(
+                        out=acc[:, e, :], lhsT=w2w[:, 2 * P * t : 2 * P * (t + 1)].bitcast(FP4X4), lhsT_scale=w2s[:, P * t : P * (t + 1)],
+                        rhs=qw[:].bitcast(FP8X4), rhs_scale=qs[:], start=True, stop=True,
+                    )
+                pair.append(acc)
+            accs.append(pair)
+
+        def add_res(c):
+            o = sb("o%d" % c, [P, PACK, CH], F32)
+            for k in range(2):
+                nc.vector.tensor_tensor(o[:, 2 * k : 2 * k + 2, :], accs[c][k][:], res_sb[c][:, 2 * k : 2 * k + 2, :], ALU.add)
+            nc.sync.dma_start(out_rows[:, :, CH * c : CH * (c + 1)], o[:])
+            outs.append(o)
+
+        n_ch = U // CH
+        for step in range(n_ch + 2):
+            if step < n_ch:
+                product(step)
+            if 1 <= step <= n_ch:
+                add_res(step - 1)
+            if step >= 2:
+                finish(step - 2)
+        for q in range(4):
+            nc.sync.dma_start(out_2[0, 4 * q : 4 * q + 4, :].bitcast(I32), o_sc[32 * q : 32 * q + 4, :].bitcast(I32))

@@ -18,7 +18,9 @@ PACK = 4
 S = 512
 HALF = 256
 U = 1024
-CH = 256
+WIDTHS = [128, 128, 256, 256, 128, 128]
+STARTS = [sum(WIDTHS[:c]) for c in range(len(WIDTHS))]
+ON_VECTOR = 2
 FLOPS = 2 * 512 * 512 * (512 + 512 + 1024)
 
 
@@ -31,8 +33,8 @@ def tile_picked_pqkkindapagez_none_po_kernel(
         keep = ctx.enter_context(tc.tile_pool(name="keep", bufs=1))
         psum = ctx.enter_context(tc.psum_pool(name="psum", bufs=8))
 
-        def sb(name, shape, dtype):
-            return keep.tile(shape, dtype, name=name, align_bytes=64)
+        def sb(name, shape, dtype, after=None):
+            return keep.tile(shape, dtype, name=name, tag=after or name, align_bytes=64)
 
         def load_list(name, src):
             lst = keep.tile([P, S // 16], U16, name=name)
@@ -48,23 +50,26 @@ def tile_picked_pqkkindapagez_none_po_kernel(
             for q in range(4):
                 nc.sync.dma_start(plane[32 * q : 32 * q + 4, :].bitcast(I32), src[0, 4 * q : 4 * q + 4, :].bitcast(I32))
 
-        def deal_fp4(name, raw_words, raw_scales):
-            words = sb(name + "_w", [P, 2 * S], U8)
+        def deal_words(name, raw_words, after=None):
+            words = sb(name, [P, 2 * S], U8, after)
             nc.vector.tensor_copy(
-                words[:].rearrange("p (t m b) -> p t m b", t=PACK, b=2),
-                raw_words[:].rearrange("p (m t b) -> p t m b", t=PACK, b=2),
+                words[:].bitcast(U16).rearrange("p (t m) -> p t m", t=PACK),
+                raw_words[:].bitcast(U16).rearrange("p (m t) -> p t m", t=PACK),
             )
-            scales = sb(name + "_s", [P, S], U8)
+            return words
+
+        def deal_scales(name, raw_scales, after=None):
+            scales = sb(name, [P, S], U8, after)
             nc.vector.tensor_copy(
                 scales[:].rearrange("p (t m) -> p t m", t=PACK),
                 raw_scales[:].rearrange("p (m t) -> p t m", t=PACK),
             )
-            return words, scales
+            return scales
 
         def interleave(dst, src):
             nc.scalar.copy(
-                dst[:].rearrange("p (c i) t -> p c t i", i=4),
-                src[:].rearrange("p t (c i) -> p c t i", i=4),
+                dst.rearrange("p (c i) t -> p c t i", i=4),
+                src.rearrange("p t (c i) -> p c t i", i=4),
             )
 
         def half_of(lst, h):
@@ -75,9 +80,9 @@ def tile_picked_pqkkindapagez_none_po_kernel(
         ds_win = zeroed_bytes("ds_win", 2048)
         w2s_raw = zeroed_bytes("w2s_raw", S)
         d_sc = zeroed_bytes("d_sc", S)
-        page = [sb("page%d" % t, [P, U], F32) for t in range(PACK)]
-        for t in range(PACK):
-            nc.gpsimd.memset(page[t][:], 0.0)
+        page = [sb("page%d" % t, [P, U], F32) for t in range(PACK - 1)]
+        for t in range(PACK - 1):
+            nc.vector.memset(page[t][:].bitcast(I32), 0)
 
         tab_rows = tab.rearrange("(p t) j -> t p j", t=PACK)
         tab_win = [sb("tab%d" % t, [P, S], F32) for t in range(PACK)]
@@ -111,9 +116,10 @@ def tile_picked_pqkkindapagez_none_po_kernel(
         nc.sync.dma_start(w2w_raw[:].bitcast(I32), w2_words[0].bitcast(I32))
         load_scale_rows(w2s_raw, w2_scales)
         res_rows = res.rearrange("(p t) w -> p t w", t=PACK)
-        res_sb = [sb("res%d" % c, [P, PACK, CH], F32) for c in range(U // CH)]
-        for c in range(U // CH):
-            nc.sync.dma_start(res_sb[c][:], res_rows[:, :, CH * c : CH * (c + 1)])
+        chunks = [slice(STARTS[c], STARTS[c] + WIDTHS[c]) for c in range(len(WIDTHS))]
+        res_sb = [sb("res%d" % c, [P, PACK, w], F32) for c, w in enumerate(WIDTHS)]
+        for c, cols in enumerate(chunks):
+            nc.sync.dma_start(res_sb[c][:], res_rows[:, :, cols])
 
         t1 = [sb("t1_%d" % t, [P, S], F32) for t in range(PACK)]
 
@@ -127,7 +133,8 @@ def tile_picked_pqkkindapagez_none_po_kernel(
         nc.vector.tensor_copy(xw[:].bitcast(U32), xw_win[:].bitcast(U32).indirect(lx[:]))
         xs = sb("xs", [P, S], U8)
         nc.vector.tensor_copy(xs[:], xs_win[:].indirect(lx[:]))
-        w1w, w1s = deal_fp4("w1", w1w_raw, w1s_raw)
+        w1w = deal_words("w1w", w1w_raw)
+        w1s = deal_scales("w1s", w1s_raw)
 
         y_win = [sb("y%d" % t, [P, S], F32) for t in range(PACK)]
         tabg = [sb("tabg%d" % t, [P, S], F32) for t in range(PACK)]
@@ -144,14 +151,13 @@ def tile_picked_pqkkindapagez_none_po_kernel(
 
         dsg = sb("dsg", [P, S], U8)
         nc.vector.tensor_copy(dsg[:], ds_win[:].indirect(lk[:]))
-        dsd = sb("dsd", [P, S], U8)
-        nc.vector.tensor_copy(dsd[:].rearrange("p (t m) -> p t m", t=PACK), dsg[:].rearrange("p (m t) -> p t m", t=PACK))
-        for r in range(4):
-            nc.sync.dma_start(d_sc[r:P:32, :].bitcast(I32), dsd[16 * (r // 2) + r % 2 : P : 32, :].bitcast(I32))
         dwg = sb("dwg", [P, S], I32)
         nc.vector.tensor_copy(dwg[:].bitcast(U32), dw_win[:].bitcast(U32).indirect(lk[:]))
+        dsd = deal_scales("dsd", dsg)
+        for r in range(4):
+            nc.sync.dma_start(d_sc[r:P:32, :].bitcast(I32), dsd[16 * (r // 2) + r % 2 : P : 32, :].bitcast(I32))
         dw = sb("dw", [P, S], I32)
-        nc.vector.tensor_copy(dw[:].rearrange("p (t m) -> p t m", t=PACK), dwg[:].rearrange("p (m t) -> p t m", t=PACK))
+        nc.vector.tensor_copy(dw[:].rearrange("p (t m) -> p m t", t=PACK), dwg[:].rearrange("p (m t) -> p m t", t=PACK))
 
         gpos = sb("gpos", [P, PACK], F32)
         nc.scalar.activation(gpos[:], gn_sb[:], ACT.Copy, scale=0.0625)
@@ -159,18 +165,29 @@ def tile_picked_pqkkindapagez_none_po_kernel(
         nc.scalar.activation(gneg[:], gn_sb[:], ACT.Copy, scale=-0.0625)
 
         s_acc = [psum.tile([P, S], F32, name="bank") for t in range(PACK)]
+        neg = [sb("neg%d" % t, [P, S], F32) for t in range(PACK)]
+        pos = [sb("pos%d" % t, [P, S], F32) for t in range(PACK)]
+
+        def negative_part(t, cols):
+            nc.scalar.activation(pos[t][:, cols], s_acc[t][:, cols], ACT.Relu)
+            nc.scalar.activation(neg[t][:, cols], pos[t][:, cols], ACT.Copy, scale=gneg[:, t : t + 1])
+
         for h in range(2):
             cols = slice(HALF * h, HALF * (h + 1))
             prod = sb("prod%d" % h, [P, PACK, HALF], F32)
             z = sb("z%d" % h, [P, PACK, HALF], F32)
+            zb = sb("zb%d" % h, [P, HALF, PACK], BF16)
             for t in range(PACK):
                 nc.vector.tensor_tensor(prod[:, t, :], y_win[t][:].indirect(half_of(l3, h)), t1[t][:, cols], ALU.mult)
             for t in range(PACK):
                 nc.vector.tensor_tensor(z[:, t, :], tabg[t][:].indirect(half_of(l2, h)), prod[:, t, :], ALU.add)
-            zb = sb("zb%d" % h, [P, HALF, PACK], BF16)
-            interleave(zb, z)
-            if h == 1:
-                w2w, w2s = deal_fp4("w2", w2w_raw, w2s_raw)
+                if h == 1 and t % 2 == 1:
+                    interleave(zb[:, :, t - 1 : t + 1], z[:, t - 1 : t + 1, :])
+            if h == 0:
+                interleave(zb[:], z[:])
+            else:
+                w2w = deal_words("w2w", w2w_raw, after="prod1")
+                w2s = deal_scales("w2s", w2s_raw, after="tabg3")
             zw = sb("zw%d" % h, [P, HALF], I32)
             zs = sb("zs%d" % h, [P, HALF], U8)
             nc.vector.quantize_mx(out=zw[:].bitcast(FP8X4), scales=zs[:], in_=zb[:].rearrange("p c t -> p (c t)"))
@@ -179,28 +196,38 @@ def tile_picked_pqkkindapagez_none_po_kernel(
                     out=s_acc[t][:, cols], lhsT=dw[:, P * t : P * (t + 1)].bitcast(FP8X4), lhsT_scale=d_sc[:, P * t : P * (t + 1)],
                     rhs=zw[:].bitcast(FP8X4), rhs_scale=zs[:], start=True, stop=True,
                 )
-
-        z2b = [sb("z2b%d" % c, [P, CH, PACK], BF16) for c in range(U // CH)]
-        for t in range(PACK):
-            neg = sb("neg%d" % t, [P, S], F32)
-            if t == 0:
-                nc.vector.tensor_scalar(neg[:], s_acc[t][:], 0.0, gneg[:, t : t + 1], ALU.max, ALU.mult)
+            if h == 0:
+                negative_part(0, cols)
             else:
-                pos = sb("pos%d" % t, [P, S], F32)
-                nc.scalar.activation(pos[:], s_acc[t][:], ACT.Relu)
-                nc.scalar.activation(neg[:], pos[:], ACT.Copy, scale=gneg[:, t : t + 1])
-            own = sb("own%d" % t, [P, S], F32)
-            nc.scalar.activation(own[:], s_acc[t][:], ACT.Copy, scale=gpos[:, t : t + 1])
-            got = sb("got%d" % t, [P, S], F32)
+                page.append(sb("page3", [P, U], F32, after="zb1"))
+                nc.vector.memset(page[3][:].bitcast(I32), 0)
+                nc.vector.tensor_scalar(neg[0][:, cols], s_acc[0][:, cols], 0.0, gneg[:, 0:1], ALU.max, ALU.mult)
+
+        z2b = [sb("z2b%d" % c, [P, w, PACK], BF16) for c, w in enumerate(WIDTHS)]
+        own = [sb("own%d" % t, [P, S], F32) for t in range(PACK)]
+        got = [sb("got%d" % t, [P, S], F32) for t in range(PACK)]
+
+        def fetch_neg(t):
+            if t > 0:
+                negative_part(t, slice(0, S))
             for h in range(2):
-                nc.vector.tensor_copy(got[:, HALF * h : HALF * (h + 1)], neg[:].indirect(half_of(l5, h)))
-            nc.vector.tensor_tensor(page[t][:].indirect(l4[:]), own[:], got[:], ALU.add)
+                nc.vector.tensor_copy(got[t][:, HALF * h : HALF * (h + 1)], neg[t][:].indirect(half_of(l5, h)))
+
+        def put(t):
+            nc.scalar.activation(own[t][:], s_acc[t][:], ACT.Copy, scale=gpos[:, t : t + 1])
+            nc.vector.tensor_tensor(page[t][:].indirect(l4[:]), own[t][:], got[t][:], ALU.add)
+
+        fetch_neg(0)
         for t in range(PACK):
-            for c in range(U // CH):
-                src = page[t][:, CH * c : CH * (c + 1)]
-                if t == 2 and c == 0:
-                    nc.scalar.copy(z2b[c][:, :, 2:4], src.unsqueeze(2).to_broadcast([P, CH, 2]))
-                elif t == 3 and c == 0:
+            if t + 1 < PACK:
+                fetch_neg(t + 1)
+            put(t)
+        for t in range(PACK):
+            for c, cols in enumerate(chunks):
+                src = page[t][:, cols]
+                if t == 2 and c < ON_VECTOR:
+                    nc.scalar.copy(z2b[c][:, :, 2:4], src.unsqueeze(2).to_broadcast([P, WIDTHS[c], 2]))
+                elif t == 3 and c < ON_VECTOR:
                     nc.vector.tensor_copy(z2b[c][:, :, t], src)
                 else:
                     nc.scalar.copy(z2b[c][:, :, t], src)
@@ -209,46 +236,50 @@ def tile_picked_pqkkindapagez_none_po_kernel(
         out_words = out_1[0].rearrange("p c r -> p (c r)").bitcast(I32)
         o_sc = sb("o_sc", [P, U], U8)
         outs = []
-
-        def finish(c):
-            ob = sb("ob%d" % c, [P, CH, PACK], BF16)
-            interleave(ob, outs[c])
-            ow = sb("ow%d" % c, [P, CH], I32)
-            nc.vector.quantize_mx(out=ow[:].bitcast(FP8X4), scales=o_sc[:, CH * c : CH * (c + 1)], in_=ob[:].rearrange("p c t -> p (c t)"))
-            nc.sync.dma_start(out_words[:, CH * c : CH * (c + 1)], ow[:])
-
         accs = []
 
         def product(c):
-            qw = sb("qw%d" % c, [P, CH], I32)
-            qs = sb("qs%d" % c, [P, CH], U8)
+            w = WIDTHS[c]
+            qw = sb("qw%d" % c, [P, w], I32)
+            qs = sb("qs%d" % c, [P, w], U8)
             nc.vector.quantize_mx(out=qw[:].bitcast(FP8X4), scales=qs[:], in_=z2b[c][:].rearrange("p c t -> p (c t)"))
-            pair = []
-            for k in range(2):
-                acc = psum.tile([P, 2, CH], F32, name="bank")
-                for e in range(2):
-                    t = 2 * k + e
+            per_bank = 512 // w
+            banks = []
+            for k in range(PACK // per_bank):
+                acc = psum.tile([P, per_bank, w], F32, name="bank")
+                for e in range(per_bank):
+                    t = per_bank * k + e
                     nc.tensor.matmul_mx(
                         out=acc[:, e, :], lhsT=w2w[:, 2 * P * t : 2 * P * (t + 1)].bitcast(FP4X4), lhsT_scale=w2s[:, P * t : P * (t + 1)],
                         rhs=qw[:].bitcast(FP8X4), rhs_scale=qs[:], start=True, stop=True,
                     )
-                pair.append(acc)
-            accs.append(pair)
+                banks.append(acc)
+            accs.append(banks)
 
         def add_res(c):
-            o = sb("o%d" % c, [P, PACK, CH], F32)
-            for k in range(2):
-                nc.vector.tensor_tensor(o[:, 2 * k : 2 * k + 2, :], accs[c][k][:], res_sb[c][:, 2 * k : 2 * k + 2, :], ALU.add)
-            nc.sync.dma_start(out_rows[:, :, CH * c : CH * (c + 1)], o[:])
+            per_bank = 512 // WIDTHS[c]
+            o = sb("o%d" % c, [P, PACK, WIDTHS[c]], F32)
+            for k, acc in enumerate(accs[c]):
+                rows = slice(per_bank * k, per_bank * (k + 1))
+                nc.vector.tensor_tensor(o[:, rows, :], acc[:], res_sb[c][:, rows, :], ALU.add)
+            nc.sync.dma_start(out_rows[:, :, chunks[c]], o[:])
             outs.append(o)
 
-        n_ch = U // CH
-        for step in range(n_ch + 2):
+        def finish(c):
+            ob = sb("ob%d" % c, [P, WIDTHS[c], PACK], BF16)
+            interleave(ob[:], outs[c][:])
+            ow = sb("ow%d" % c, [P, WIDTHS[c]], I32)
+            nc.vector.quantize_mx(out=ow[:].bitcast(FP8X4), scales=o_sc[:, chunks[c]], in_=ob[:].rearrange("p c t -> p (c t)"))
+            nc.sync.dma_start(out_words[:, chunks[c]], ow[:])
+
+        n_ch = len(WIDTHS)
+        for step in range(n_ch + 5):
             if step < n_ch:
                 product(step)
-            if 1 <= step <= n_ch:
-                add_res(step - 1)
-            if step >= 2:
-                finish(step - 2)
+            if 2 <= step < n_ch + 2:
+                add_res(step - 2)
+            if step >= 5:
+                finish(step - 5)
         for q in range(4):
-            nc.sync.dma_start(out_2[0, 4 * q : 4 * q + 4, :].bitcast(I32), o_sc[32 * q : 32 * q + 4, :].bitcast(I32))
+            queue = nc.sync if q % 2 else nc.scalar
+            queue.dma_start(out_2[0, 4 * q : 4 * q + 4, :].bitcast(I32), o_sc[32 * q : 32 * q + 4, :].bitcast(I32))

@@ -80,15 +80,16 @@ def tile_picked_pqkkindapagez_none_po_kernel(
         ds_win = zeroed_bytes("ds_win", 2048)
         w2s_raw = zeroed_bytes("w2s_raw", S)
         d_sc = zeroed_bytes("d_sc", S)
-        page = [sb("page%d" % t, [P, U], F32) for t in range(PACK - 1)]
-        for t in range(PACK - 1):
+        page = [sb("page%d" % t, [P, U], F32) for t in range(2)]
+        for t in range(2):
             nc.vector.memset(page[t][:].bitcast(I32), 0)
 
         tab_rows = tab.rearrange("(p t) j -> t p j", t=PACK)
-        tab_win = [sb("tab%d" % t, [P, S], F32) for t in range(PACK)]
+        tab_win = [sb("tab%d" % t, [P, 2 * S], F32) for t in range(PACK)]
+        nc.sync.dma_start(tab_win[0][:, :S], tab_rows[0])
         l1 = load_list("l1", n1)
-        nc.sync.dma_start(tab_win[0][:], tab_rows[0])
-        nc.sync.dma_start(tab_win[1][:], tab_rows[1])
+        for t in range(1, PACK):
+            nc.sync.dma_start(tab_win[t][:, :S], tab_rows[t])
         lx = load_list("lx", offs)
         xw_win = sb("xw_win", [P, 1024], I32)
         nc.sync.dma_start(xw_win[:], x_words[0].rearrange("p c r -> p (c r)").bitcast(I32))
@@ -96,18 +97,16 @@ def tile_picked_pqkkindapagez_none_po_kernel(
         nc.sync.dma_start(w1w_raw[:].bitcast(I32), w1_words[0].bitcast(I32))
         load_scale_rows(xs_win, x_scales)
         load_scale_rows(w1s_raw, w1_scales)
-        nc.sync.dma_start(tab_win[2][:], tab_rows[2])
-        nc.sync.dma_start(tab_win[3][:], tab_rows[3])
+        lk = load_list("lk", kidx)
         gs_sb = sb("gs_sb", [P, PACK], F32)
         nc.sync.dma_start(gs_sb[:], gs.rearrange("(p t) o -> p (t o)", t=PACK))
-        lk = load_list("lk", kidx)
         d_rows = d_scales[0].rearrange("(r e) c -> e r c", e=2)
         for e in range(2):
             nc.sync.dma_start(ds_win[e:P:16, :].bitcast(I32), d_rows[e].bitcast(I32))
-        l3 = load_list("l3", n3)
-        l2 = load_list("l2", n2)
         dw_win = sb("dw_win", [P, 2048], I32)
         nc.sync.dma_start(dw_win[:], d_words[0].rearrange("p c r -> p (c r)").bitcast(I32))
+        l3 = load_list("l3", n3)
+        l2 = load_list("l2", n2)
         gn_sb = sb("gn_sb", [P, PACK], F32)
         nc.sync.dma_start(gn_sb[:], gn.rearrange("(p t) o -> p (t o)", t=PACK))
         l5 = load_list("l5", n5)
@@ -124,11 +123,10 @@ def tile_picked_pqkkindapagez_none_po_kernel(
         t1 = [sb("t1_%d" % t, [P, S], F32) for t in range(PACK)]
 
         def fetch_t1(t):
-            for h in range(2):
-                nc.vector.tensor_copy(t1[t][:, HALF * h : HALF * (h + 1)], tab_win[t][:].indirect(half_of(l1, h)))
+            nc.vector.tensor_copy(t1[t][:], tab_win[t][:].indirect(l1[:]))
 
-        fetch_t1(0)
-        fetch_t1(1)
+        for t in range(PACK):
+            fetch_t1(t)
         xw = sb("xw", [P, S], I32)
         nc.vector.tensor_copy(xw[:].bitcast(U32), xw_win[:].bitcast(U32).indirect(lx[:]))
         xs = sb("xs", [P, S], U8)
@@ -136,7 +134,7 @@ def tile_picked_pqkkindapagez_none_po_kernel(
         w1w = deal_words("w1w", w1w_raw)
         w1s = deal_scales("w1s", w1s_raw)
 
-        y_win = [sb("y%d" % t, [P, S], F32) for t in range(PACK)]
+        y_win = [sb("y%d" % t, [P, 2 * S], F32) for t in range(PACK)]
         tabg = [sb("tabg%d" % t, [P, S], F32) for t in range(PACK)]
         for t in range(PACK):
             acc = psum.tile([P, S], F32, name="bank")
@@ -144,10 +142,8 @@ def tile_picked_pqkkindapagez_none_po_kernel(
                 out=acc[:], lhsT=w1w[:, 2 * P * t : 2 * P * (t + 1)].bitcast(FP4X4), lhsT_scale=w1s[:, P * t : P * (t + 1)],
                 rhs=xw[:].bitcast(FP8X4), rhs_scale=xs[:], start=True, stop=True,
             )
-            nc.scalar.activation(y_win[t][:], acc[:], ACT.Copy, scale=gs_sb[:, t : t + 1])
-            nc.scalar.activation(tabg[t][:], tab_win[t][:], ACT.Copy, scale=gs_sb[:, t : t + 1])
-        fetch_t1(2)
-        fetch_t1(3)
+            nc.scalar.activation(y_win[t][:, :S], acc[:], ACT.Copy, scale=gs_sb[:, t : t + 1])
+            nc.scalar.activation(tabg[t][:], tab_win[t][:, :S], ACT.Copy, scale=gs_sb[:, t : t + 1])
 
         dsg = sb("dsg", [P, S], U8)
         nc.vector.tensor_copy(dsg[:], ds_win[:].indirect(lk[:]))
@@ -165,29 +161,31 @@ def tile_picked_pqkkindapagez_none_po_kernel(
         nc.scalar.activation(gneg[:], gn_sb[:], ACT.Copy, scale=-0.0625)
 
         s_acc = [psum.tile([P, S], F32, name="bank") for t in range(PACK)]
-        neg = [sb("neg%d" % t, [P, S], F32) for t in range(PACK)]
+        neg = [sb("neg%d" % t, [P, 2 * S], F32) for t in range(PACK)]
         pos = [sb("pos%d" % t, [P, S], F32) for t in range(PACK)]
 
         def negative_part(t, cols):
             nc.scalar.activation(pos[t][:, cols], s_acc[t][:, cols], ACT.Relu)
             nc.scalar.activation(neg[t][:, cols], pos[t][:, cols], ACT.Copy, scale=gneg[:, t : t + 1])
 
+        prod = sb("prod", [P, PACK, S], F32)
+        for t in range(PACK):
+            nc.vector.tensor_tensor(prod[:, t, :], y_win[t][:].indirect(l3[:]), t1[t][:], ALU.mult)
         for h in range(2):
             cols = slice(HALF * h, HALF * (h + 1))
-            prod = sb("prod%d" % h, [P, PACK, HALF], F32)
             z = sb("z%d" % h, [P, PACK, HALF], F32)
             zb = sb("zb%d" % h, [P, HALF, PACK], BF16)
             for t in range(PACK):
-                nc.vector.tensor_tensor(prod[:, t, :], y_win[t][:].indirect(half_of(l3, h)), t1[t][:, cols], ALU.mult)
-            for t in range(PACK):
-                nc.vector.tensor_tensor(z[:, t, :], tabg[t][:].indirect(half_of(l2, h)), prod[:, t, :], ALU.add)
+                nc.vector.tensor_tensor(z[:, t, :], tabg[t][:].indirect(half_of(l2, h)), prod[:, t, cols], ALU.add)
                 if h == 1 and t % 2 == 1:
                     interleave(zb[:, :, t - 1 : t + 1], z[:, t - 1 : t + 1, :])
             if h == 0:
                 interleave(zb[:], z[:])
             else:
-                w2w = deal_words("w2w", w2w_raw, after="prod1")
+                w2w = deal_words("w2w", w2w_raw, after="prod")
                 w2s = deal_scales("w2s", w2s_raw, after="tabg3")
+                page.append(sb("page2", [P, U], F32, after="tabg2"))
+                nc.vector.memset(page[2][:].bitcast(I32), 0)
             zw = sb("zw%d" % h, [P, HALF], I32)
             zs = sb("zs%d" % h, [P, HALF], U8)
             nc.vector.quantize_mx(out=zw[:].bitcast(FP8X4), scales=zs[:], in_=zb[:].rearrange("p c t -> p (c t)"))
@@ -210,18 +208,20 @@ def tile_picked_pqkkindapagez_none_po_kernel(
         def fetch_neg(t):
             if t > 0:
                 negative_part(t, slice(0, S))
-            for h in range(2):
-                nc.vector.tensor_copy(got[t][:, HALF * h : HALF * (h + 1)], neg[t][:].indirect(half_of(l5, h)))
+            nc.vector.tensor_copy(got[t][:], neg[t][:].indirect(l5[:]))
 
         def put(t):
             nc.scalar.activation(own[t][:], s_acc[t][:], ACT.Copy, scale=gpos[:, t : t + 1])
             nc.vector.tensor_tensor(page[t][:].indirect(l4[:]), own[t][:], got[t][:], ALU.add)
 
         fetch_neg(0)
-        for t in range(PACK):
-            if t + 1 < PACK:
-                fetch_neg(t + 1)
-            put(t)
+        fetch_neg(1)
+        put(0)
+        fetch_neg(2)
+        put(1)
+        put(2)
+        fetch_neg(3)
+        put(3)
         for t in range(PACK):
             for c, cols in enumerate(chunks):
                 src = page[t][:, cols]
@@ -235,12 +235,14 @@ def tile_picked_pqkkindapagez_none_po_kernel(
         out_rows = out_0.rearrange("(p t) w -> p t w", t=PACK)
         out_words = out_1[0].rearrange("p c r -> p (c r)").bitcast(I32)
         o_sc = sb("o_sc", [P, U], U8)
+        o_w = sb("o_w", [P, U], I32)
+        first_out = sb("first_out", [P, PACK, STARTS[2]], F32)
         outs = []
         accs = []
 
         def product(c):
             w = WIDTHS[c]
-            qw = sb("qw%d" % c, [P, w], I32)
+            qw = sb("qw%d" % c, [P, w], I32, after="res%d" % (c - 3) if c >= 3 else None)
             qs = sb("qs%d" % c, [P, w], U8)
             nc.vector.quantize_mx(out=qw[:].bitcast(FP8X4), scales=qs[:], in_=z2b[c][:].rearrange("p c t -> p (c t)"))
             per_bank = 512 // w
@@ -258,19 +260,27 @@ def tile_picked_pqkkindapagez_none_po_kernel(
 
         def add_res(c):
             per_bank = 512 // WIDTHS[c]
-            o = sb("o%d" % c, [P, PACK, WIDTHS[c]], F32)
+            if c < 2:
+                o = first_out[:, :, chunks[c]]
+            else:
+                o = sb("o%d" % c, [P, PACK, WIDTHS[c]], F32)[:]
             for k, acc in enumerate(accs[c]):
                 rows = slice(per_bank * k, per_bank * (k + 1))
                 nc.vector.tensor_tensor(o[:, rows, :], acc[:], res_sb[c][:, rows, :], ALU.add)
-            nc.sync.dma_start(out_rows[:, :, chunks[c]], o[:])
+            if c == 1:
+                nc.sync.dma_start(out_rows[:, :, : STARTS[2]], first_out[:])
+            elif c > 1:
+                nc.sync.dma_start(out_rows[:, :, chunks[c]], o)
             outs.append(o)
 
         def finish(c):
             ob = sb("ob%d" % c, [P, WIDTHS[c], PACK], BF16)
-            interleave(ob[:], outs[c][:])
-            ow = sb("ow%d" % c, [P, WIDTHS[c]], I32)
-            nc.vector.quantize_mx(out=ow[:].bitcast(FP8X4), scales=o_sc[:, chunks[c]], in_=ob[:].rearrange("p c t -> p (c t)"))
-            nc.sync.dma_start(out_words[:, chunks[c]], ow[:])
+            interleave(ob[:], outs[c])
+            nc.vector.quantize_mx(out=o_w[:, chunks[c]].bitcast(FP8X4), scales=o_sc[:, chunks[c]], in_=ob[:].rearrange("p c t -> p (c t)"))
+            if c == 3:
+                nc.sync.dma_start(out_words[:, : STARTS[4]], o_w[:, : STARTS[4]])
+            elif c == 5:
+                nc.sync.dma_start(out_words[:, STARTS[4] :], o_w[:, STARTS[4] :])
 
         n_ch = len(WIDTHS)
         for step in range(n_ch + 5):

@@ -18,9 +18,9 @@ PACK = 4
 S = 512
 HALF = 256
 U = 1024
-WIDTHS = [128, 128, 256, 256, 128, 128]
+WIDTHS = [256, 256, 256, 128, 128]
 STARTS = [sum(WIDTHS[:c]) for c in range(len(WIDTHS))]
-ON_VECTOR = 2
+ON_VECTOR = 1
 FLOPS = 2 * 512 * 512 * (512 + 512 + 1024)
 
 
@@ -43,7 +43,7 @@ def tile_picked_pqkkindapagez_none_po_kernel(
 
         def zeroed_bytes(name, width):
             plane = sb(name, [P, width], U8)
-            nc.vector.memset(plane[:].bitcast(I32), 0)
+            nc.gpsimd.memset(plane[:].bitcast(I32), 0)
             return plane
 
         def load_scale_rows(plane, src):
@@ -80,9 +80,9 @@ def tile_picked_pqkkindapagez_none_po_kernel(
         ds_win = zeroed_bytes("ds_win", 2048)
         w2s_raw = zeroed_bytes("w2s_raw", S)
         d_sc = zeroed_bytes("d_sc", S)
-        page = [sb("page%d" % t, [P, U], F32) for t in range(2)]
-        for t in range(2):
-            nc.vector.memset(page[t][:].bitcast(I32), 0)
+        page = [sb("page%d" % t, [P, U], F32) for t in range(PACK)]
+        for t in range(PACK):
+            nc.gpsimd.memset(page[t][:], 0.0)
 
         tab_rows = tab.rearrange("(p t) j -> t p j", t=PACK)
         tab_win = [sb("tab%d" % t, [P, 2 * S], F32) for t in range(PACK)]
@@ -103,10 +103,10 @@ def tile_picked_pqkkindapagez_none_po_kernel(
         d_rows = d_scales[0].rearrange("(r e) c -> e r c", e=2)
         for e in range(2):
             nc.sync.dma_start(ds_win[e:P:16, :].bitcast(I32), d_rows[e].bitcast(I32))
-        dw_win = sb("dw_win", [P, 2048], I32)
-        nc.sync.dma_start(dw_win[:], d_words[0].rearrange("p c r -> p (c r)").bitcast(I32))
         l3 = load_list("l3", n3)
         l2 = load_list("l2", n2)
+        dw_win = sb("dw_win", [P, 2048], I32)
+        nc.sync.dma_start(dw_win[:], d_words[0].rearrange("p c r -> p (c r)").bitcast(I32))
         gn_sb = sb("gn_sb", [P, PACK], F32)
         nc.sync.dma_start(gn_sb[:], gn.rearrange("(p t) o -> p (t o)", t=PACK))
         l5 = load_list("l5", n5)
@@ -147,13 +147,9 @@ def tile_picked_pqkkindapagez_none_po_kernel(
 
         dsg = sb("dsg", [P, S], U8)
         nc.vector.tensor_copy(dsg[:], ds_win[:].indirect(lk[:]))
-        dwg = sb("dwg", [P, S], I32)
-        nc.vector.tensor_copy(dwg[:].bitcast(U32), dw_win[:].bitcast(U32).indirect(lk[:]))
         dsd = deal_scales("dsd", dsg)
         for r in range(4):
             nc.sync.dma_start(d_sc[r:P:32, :].bitcast(I32), dsd[16 * (r // 2) + r % 2 : P : 32, :].bitcast(I32))
-        dw = sb("dw", [P, S], I32)
-        nc.vector.tensor_copy(dw[:].rearrange("p (t m) -> p m t", t=PACK), dwg[:].rearrange("p (m t) -> p m t", t=PACK))
 
         gpos = sb("gpos", [P, PACK], F32)
         nc.scalar.activation(gpos[:], gn_sb[:], ACT.Copy, scale=0.0625)
@@ -164,42 +160,41 @@ def tile_picked_pqkkindapagez_none_po_kernel(
         neg = [sb("neg%d" % t, [P, 2 * S], F32) for t in range(PACK)]
         pos = [sb("pos%d" % t, [P, S], F32) for t in range(PACK)]
 
-        def negative_part(t, cols):
-            nc.scalar.activation(pos[t][:, cols], s_acc[t][:, cols], ACT.Relu)
-            nc.scalar.activation(neg[t][:, cols], pos[t][:, cols], ACT.Copy, scale=gneg[:, t : t + 1])
+        def negative_part(t):
+            nc.scalar.activation(pos[t][:], s_acc[t][:], ACT.Relu)
+            nc.scalar.activation(neg[t][:, :S], pos[t][:], ACT.Copy, scale=gneg[:, t : t + 1])
 
         prod = sb("prod", [P, PACK, S], F32)
         for t in range(PACK):
             nc.vector.tensor_tensor(prod[:, t, :], y_win[t][:].indirect(l3[:]), t1[t][:], ALU.mult)
+        zb = [sb("zb%d" % h, [P, HALF, PACK], BF16) for h in range(2)]
         for h in range(2):
             cols = slice(HALF * h, HALF * (h + 1))
             z = sb("z%d" % h, [P, PACK, HALF], F32)
-            zb = sb("zb%d" % h, [P, HALF, PACK], BF16)
             for t in range(PACK):
                 nc.vector.tensor_tensor(z[:, t, :], tabg[t][:].indirect(half_of(l2, h)), prod[:, t, cols], ALU.add)
-                if h == 1 and t % 2 == 1:
-                    interleave(zb[:, :, t - 1 : t + 1], z[:, t - 1 : t + 1, :])
-            if h == 0:
-                interleave(zb[:], z[:])
-            else:
-                w2w = deal_words("w2w", w2w_raw, after="prod")
-                w2s = deal_scales("w2s", w2s_raw, after="tabg3")
-                page.append(sb("page2", [P, U], F32, after="tabg2"))
-                nc.vector.memset(page[2][:].bitcast(I32), 0)
-            zw = sb("zw%d" % h, [P, HALF], I32)
-            zs = sb("zs%d" % h, [P, HALF], U8)
-            nc.vector.quantize_mx(out=zw[:].bitcast(FP8X4), scales=zs[:], in_=zb[:].rearrange("p c t -> p (c t)"))
-            for t in range(PACK):
-                nc.tensor.matmul_mx(
-                    out=s_acc[t][:, cols], lhsT=dw[:, P * t : P * (t + 1)].bitcast(FP8X4), lhsT_scale=d_sc[:, P * t : P * (t + 1)],
-                    rhs=zw[:].bitcast(FP8X4), rhs_scale=zs[:], start=True, stop=True,
-                )
-            if h == 0:
-                negative_part(0, cols)
-            else:
-                page.append(sb("page3", [P, U], F32, after="zb1"))
-                nc.vector.memset(page[3][:].bitcast(I32), 0)
-                nc.vector.tensor_scalar(neg[0][:, cols], s_acc[0][:, cols], 0.0, gneg[:, 0:1], ALU.max, ALU.mult)
+            interleave(zb[h][:], z[:])
+        zw = sb("zw", [P, S], I32)
+        zs = sb("zs", [P, S], U8)
+
+        def quantise_z(h):
+            cols = slice(HALF * h, HALF * (h + 1))
+            nc.vector.quantize_mx(out=zw[:, cols].bitcast(FP8X4), scales=zs[:, cols], in_=zb[h][:].rearrange("p c t -> p (c t)"))
+
+        dwg = sb("dwg", [P, S], I32, after="prod")
+        nc.vector.tensor_copy(dwg[:].bitcast(U32), dw_win[:].bitcast(U32).indirect(lk[:]))
+        quantise_z(0)
+        dw = sb("dw", [P, S], I32)
+        nc.vector.tensor_copy(dw[:].rearrange("p (t m) -> p m t", t=PACK), dwg[:].rearrange("p (m t) -> p m t", t=PACK))
+        quantise_z(1)
+        for t in range(PACK):
+            nc.tensor.matmul_mx(
+                out=s_acc[t][:], lhsT=dw[:, P * t : P * (t + 1)].bitcast(FP8X4), lhsT_scale=d_sc[:, P * t : P * (t + 1)],
+                rhs=zw[:].bitcast(FP8X4), rhs_scale=zs[:], start=True, stop=True,
+            )
+        w2w = deal_words("w2w", w2w_raw, after="zb0")
+        w2s = deal_scales("w2s", w2s_raw, after="zb1")
+        nc.vector.tensor_scalar(neg[0][:, :S], s_acc[0][:], 0.0, gneg[:, 0:1], ALU.max, ALU.mult)
 
         z2b = [sb("z2b%d" % c, [P, w, PACK], BF16) for c, w in enumerate(WIDTHS)]
         own = [sb("own%d" % t, [P, S], F32) for t in range(PACK)]
@@ -207,7 +202,7 @@ def tile_picked_pqkkindapagez_none_po_kernel(
 
         def fetch_neg(t):
             if t > 0:
-                negative_part(t, slice(0, S))
+                negative_part(t)
             nc.vector.tensor_copy(got[t][:], neg[t][:].indirect(l5[:]))
 
         def put(t):
@@ -236,14 +231,13 @@ def tile_picked_pqkkindapagez_none_po_kernel(
         out_words = out_1[0].rearrange("p c r -> p (c r)").bitcast(I32)
         o_sc = sb("o_sc", [P, U], U8)
         o_w = sb("o_w", [P, U], I32)
-        first_out = sb("first_out", [P, PACK, STARTS[2]], F32)
         outs = []
         accs = []
 
         def product(c):
             w = WIDTHS[c]
-            qw = sb("qw%d" % c, [P, w], I32, after="res%d" % (c - 3) if c >= 3 else None)
-            qs = sb("qs%d" % c, [P, w], U8)
+            qw = sb("qw%d" % c, [P, w], I32, after="res0" if c == 3 else None)
+            qs = sb("qs%d" % c, [P, w], U8, after="z2b3" if c == 4 else None)
             nc.vector.quantize_mx(out=qw[:].bitcast(FP8X4), scales=qs[:], in_=z2b[c][:].rearrange("p c t -> p (c t)"))
             per_bank = 512 // w
             banks = []
@@ -260,36 +254,35 @@ def tile_picked_pqkkindapagez_none_po_kernel(
 
         def add_res(c):
             per_bank = 512 // WIDTHS[c]
-            if c < 2:
-                o = first_out[:, :, chunks[c]]
-            else:
-                o = sb("o%d" % c, [P, PACK, WIDTHS[c]], F32)[:]
+            o = sb("o%d" % c, [P, PACK, WIDTHS[c]], F32)[:]
             for k, acc in enumerate(accs[c]):
                 rows = slice(per_bank * k, per_bank * (k + 1))
                 nc.vector.tensor_tensor(o[:, rows, :], acc[:], res_sb[c][:, rows, :], ALU.add)
-            if c == 1:
-                nc.sync.dma_start(out_rows[:, :, : STARTS[2]], first_out[:])
-            elif c > 1:
-                nc.sync.dma_start(out_rows[:, :, chunks[c]], o)
+            nc.sync.dma_start(out_rows[:, :, chunks[c]], o)
             outs.append(o)
 
         def finish(c):
             ob = sb("ob%d" % c, [P, WIDTHS[c], PACK], BF16)
             interleave(ob[:], outs[c])
             nc.vector.quantize_mx(out=o_w[:, chunks[c]].bitcast(FP8X4), scales=o_sc[:, chunks[c]], in_=ob[:].rearrange("p c t -> p (c t)"))
-            if c == 3:
-                nc.sync.dma_start(out_words[:, : STARTS[4]], o_w[:, : STARTS[4]])
-            elif c == 5:
-                nc.sync.dma_start(out_words[:, STARTS[4] :], o_w[:, STARTS[4] :])
+            if c == 2:
+                nc.sync.dma_start(out_words[:, : STARTS[3]], o_w[:, : STARTS[3]])
+            elif c == 4:
+                nc.sync.dma_start(out_words[:, STARTS[3] :], o_w[:, STARTS[3] :])
 
-        n_ch = len(WIDTHS)
-        for step in range(n_ch + 5):
-            if step < n_ch:
-                product(step)
-            if 2 <= step < n_ch + 2:
-                add_res(step - 2)
-            if step >= 5:
-                finish(step - 5)
+        for c in range(3):
+            product(c)
+        add_res(0)
+        product(3)
+        product(4)
+        add_res(1)
+        finish(0)
+        add_res(2)
+        finish(1)
+        add_res(3)
+        add_res(4)
+        for c in range(2, 5):
+            finish(c)
         for q in range(4):
             queue = nc.sync if q % 2 else nc.scalar
             queue.dma_start(out_2[0, 4 * q : 4 * q + 4, :].bitcast(I32), o_sc[32 * q : 32 * q + 4, :].bitcast(I32))

from contextlib import ExitStack

import concourse.mybir as mybir

F32 = mybir.dt.float32
BF16 = mybir.dt.bfloat16
I32 = mybir.dt.int32
U32 = mybir.dt.uint32
U16 = mybir.dt.uint16
U8 = mybir.dt.uint8
FP8X4 = mybir.dt.float8_e4m3fn_x4
FP4X4 = mybir.dt.float4_e2m1fn_x4
ALU = mybir.AluOpType
ACT = mybir.ActivationFunctionType

P = 128
PACK = 4
S = 512
HALF = 256
U = 1024
WIDTHS = [256, 256, 256, 128, 128]
STARTS = [sum(WIDTHS[:c]) for c in range(len(WIDTHS))]
ON_VECTOR = 1
FLOPS = 2 * 512 * 512 * (512 + 512 + 1024)


def tile_picked_pqkkindapagez_none_po_kernel(
    tc, x_words, x_scales, w1_words, w1_scales, tab, gs, d_words, d_scales, res, gn, w2_words, w2_scales,
    offs, n1, n2, n3, kidx, n4, n5, out_0, out_1, out_2,
):
    nc = tc.nc
    with ExitStack() as ctx:
        keep = ctx.enter_context(tc.tile_pool(name="keep", bufs=1))
        psum = ctx.enter_context(tc.psum_pool(name="psum", bufs=8))

        def sb(name, shape, dtype, after=None):
            return keep.tile(shape, dtype, name=name, tag=after or name, align_bytes=64)

        def load_list(name, src):
            lst = keep.tile([P, S // 16], U16, name=name)
            nc.sync.dma_start(lst[:], src)
            return lst

        def zeroed_bytes(name, width):
            plane = sb(name, [P, width], U8)
            nc.gpsimd.memset(plane[:].bitcast(I32), 0)
            return plane

        def load_scale_rows(plane, src):
            for q in range(4):
                nc.sync.dma_start(plane[32 * q : 32 * q + 4, :].bitcast(I32), src[0, 4 * q : 4 * q + 4, :].bitcast(I32))

        def deal_words(name, raw_words, after=None):
            words = sb(name, [P, 2 * S], U8, after)
            nc.vector.tensor_copy(
                words[:].bitcast(U16).rearrange("p (t m) -> p t m", t=PACK),
                raw_words[:].bitcast(U16).rearrange("p (m t) -> p t m", t=PACK),
            )
            return words

        def deal_scales(name, raw_scales, after=None):
            scales = sb(name, [P, S], U8, after)
            nc.vector.tensor_copy(
                scales[:].rearrange("p (t m) -> p t m", t=PACK),
                raw_scales[:].rearrange("p (m t) -> p t m", t=PACK),
            )
            return scales

        def interleave(dst, src):
            nc.scalar.copy(
                dst.rearrange("p (c i) t -> p c t i", i=4),
                src.rearrange("p t (c i) -> p c t i", i=4),
            )

        def half_of(lst, h):
            return lst[:, 16 * h : 16 * (h + 1)]

        xs_win = zeroed_bytes("xs_win", 1024)
        w1s_raw = zeroed_bytes("w1s_raw", S)
        ds_win = zeroed_bytes("ds_win", 2048)
        w2s_raw = zeroed_bytes("w2s_raw", S)
        d_sc = zeroed_bytes("d_sc", S)
        page = [sb("page%d" % t, [P, U], F32) for t in range(PACK)]
        for t in range(PACK):
            nc.gpsimd.memset(page[t][:], 0.0)

        tab_rows = tab.rearrange("(p t) j -> t p j", t=PACK)
        tab_win = [sb("tab%d" % t, [P, 2 * S], F32) for t in range(PACK)]
        nc.sync.dma_start(tab_win[0][:, :S], tab_rows[0])
        l1 = load_list("l1", n1)
        for t in range(1, PACK):
            nc.sync.dma_start(tab_win[t][:, :S], tab_rows[t])
        lx = load_list("lx", offs)
        xw_win = sb("xw_win", [P, 1024], I32)
        nc.sync.dma_start(xw_win[:], x_words[0].rearrange("p c r -> p (c r)").bitcast(I32))
        w1w_raw = sb("w1w_raw", [P, 2 * S], U8)
        nc.sync.dma_start(w1w_raw[:].bitcast(I32), w1_words[0].bitcast(I32))
        load_scale_rows(xs_win, x_scales)
        load_scale_rows(w1s_raw, w1_scales)
        lk = load_list("lk", kidx)
        gs_sb = sb("gs_sb", [P, PACK], F32)
        nc.sync.dma_start(gs_sb[:], gs.rearrange("(p t) o -> p (t o)", t=PACK))
        d_rows = d_scales[0].rearrange("(r e) c -> e r c", e=2)
        for e in range(2):
            nc.sync.dma_start(ds_win[e:P:16, :].bitcast(I32), d_rows[e].bitcast(I32))
        l3 = load_list("l3", n3)
        l2 = load_list("l2", n2)
        dw_win = sb("dw_win", [P, 2048], I32)
        nc.sync.dma_start(dw_win[:], d_words[0].rearrange("p c r -> p (c r)").bitcast(I32))
        gn_sb = sb("gn_sb", [P, PACK], F32)
        nc.sync.dma_start(gn_sb[:], gn.rearrange("(p t) o -> p (t o)", t=PACK))
        l5 = load_list("l5", n5)
        l4 = load_list("l4", n4)
        w2w_raw = sb("w2w_raw", [P, 2 * S], U8)
        nc.sync.dma_start(w2w_raw[:].bitcast(I32), w2_words[0].bitcast(I32))
        load_scale_rows(w2s_raw, w2_scales)
        res_rows = res.rearrange("(p t) w -> p t w", t=PACK)
        chunks = [slice(STARTS[c], STARTS[c] + WIDTHS[c]) for c in range(len(WIDTHS))]
        res_sb = [sb("res%d" % c, [P, PACK, w], F32) for c, w in enumerate(WIDTHS)]
        for c, cols in enumerate(chunks):
            nc.sync.dma_start(res_sb[c][:], res_rows[:, :, cols])

        t1 = [sb("t1_%d" % t, [P, S], F32) for t in range(PACK)]

        def fetch_t1(t):
            nc.vector.tensor_copy(t1[t][:], tab_win[t][:].indirect(l1[:]))

        for t in range(PACK):
            fetch_t1(t)
        xw = sb("xw", [P, S], I32)
        nc.vector.tensor_copy(xw[:].bitcast(U32), xw_win[:].bitcast(U32).indirect(lx[:]))
        xs = sb("xs", [P, S], U8)
        nc.vector.tensor_copy(xs[:], xs_win[:].indirect(lx[:]))
        w1w = deal_words("w1w", w1w_raw)
        w1s = deal_scales("w1s", w1s_raw)

        y_win = [sb("y%d" % t, [P, 2 * S], F32) for t in range(PACK)]
        tabg = [sb("tabg%d" % t, [P, S], F32) for t in range(PACK)]
        for t in range(PACK):
            acc = psum.tile([P, S], F32, name="bank")
            nc.tensor.matmul_mx(
                out=acc[:], lhsT=w1w[:, 2 * P * t : 2 * P * (t + 1)].bitcast(FP4X4), lhsT_scale=w1s[:, P * t : P * (t + 1)],
                rhs=xw[:].bitcast(FP8X4), rhs_scale=xs[:], start=True, stop=True,
            )
            nc.scalar.activation(y_win[t][:, :S], acc[:], ACT.Copy, scale=gs_sb[:, t : t + 1])
            nc.scalar.activation(tabg[t][:], tab_win[t][:, :S], ACT.Copy, scale=gs_sb[:, t : t + 1])

        dsg = sb("dsg", [P, S], U8)
        nc.vector.tensor_copy(dsg[:], ds_win[:].indirect(lk[:]))
        dsd = deal_scales("dsd", dsg)
        for r in range(4):
            nc.sync.dma_start(d_sc[r:P:32, :].bitcast(I32), dsd[16 * (r // 2) + r % 2 : P : 32, :].bitcast(I32))

        gpos = sb("gpos", [P, PACK], F32)
        nc.scalar.activation(gpos[:], gn_sb[:], ACT.Copy, scale=0.0625)
        gneg = sb("gneg", [P, PACK], F32)
        nc.scalar.activation(gneg[:], gn_sb[:], ACT.Copy, scale=-0.0625)

        s_acc = [psum.tile([P, S], F32, name="bank") for t in range(PACK)]
        neg = [sb("neg%d" % t, [P, 2 * S], F32) for t in range(PACK)]
        pos = [sb("pos%d" % t, [P, S], F32) for t in range(PACK)]

        def negative_part(t):
            nc.scalar.activation(pos[t][:], s_acc[t][:], ACT.Relu)
            nc.scalar.activation(neg[t][:, :S], pos[t][:], ACT.Copy, scale=gneg[:, t : t + 1])

        prod = sb("prod", [P, PACK, S], F32)
        for t in range(PACK):
            nc.vector.tensor_tensor(prod[:, t, :], y_win[t][:].indirect(l3[:]), t1[t][:], ALU.mult)
        zb = [sb("zb%d" % h, [P, HALF, PACK], BF16) for h in range(2)]
        for h in range(2):
            cols = slice(HALF * h, HALF * (h + 1))
            z = sb("z%d" % h, [P, PACK, HALF], F32)
            for t in range(PACK):
                nc.vector.tensor_tensor(z[:, t, :], tabg[t][:].indirect(half_of(l2, h)), prod[:, t, cols], ALU.add)
            interleave(zb[h][:], z[:])
        zw = sb("zw", [P, S], I32)
        zs = sb("zs", [P, S], U8)

        def quantise_z(h):
            cols = slice(HALF * h, HALF * (h + 1))
            nc.vector.quantize_mx(out=zw[:, cols].bitcast(FP8X4), scales=zs[:, cols], in_=zb[h][:].rearrange("p c t -> p (c t)"))

        dwg = sb("dwg", [P, S], I32, after="prod")
        nc.vector.tensor_copy(dwg[:].bitcast(U32), dw_win[:].bitcast(U32).indirect(lk[:]))
        quantise_z(0)
        dw = sb("dw", [P, S], I32)
        nc.vector.tensor_copy(dw[:].rearrange("p (t m) -> p m t", t=PACK), dwg[:].rearrange("p (m t) -> p m t", t=PACK))
        quantise_z(1)
        for t in range(PACK):
            nc.tensor.matmul_mx(
                out=s_acc[t][:], lhsT=dw[:, P * t : P * (t + 1)].bitcast(FP8X4), lhsT_scale=d_sc[:, P * t : P * (t + 1)],
                rhs=zw[:].bitcast(FP8X4), rhs_scale=zs[:], start=True, stop=True,
            )
        w2w = deal_words("w2w", w2w_raw, after="zb0")
        w2s = deal_scales("w2s", w2s_raw, after="zb1")
        nc.vector.tensor_scalar(neg[0][:, :S], s_acc[0][:], 0.0, gneg[:, 0:1], ALU.max, ALU.mult)

        z2b = [sb("z2b%d" % c, [P, w, PACK], BF16) for c, w in enumerate(WIDTHS)]
        own = [sb("own%d" % t, [P, S], F32) for t in range(PACK)]
        got = [sb("got%d" % t, [P, S], F32) for t in range(PACK)]

        def fetch_neg(t):
            if t > 0:
                negative_part(t)
            nc.vector.tensor_copy(got[t][:], neg[t][:].indirect(l5[:]))

        def put(t):
            nc.scalar.activation(own[t][:], s_acc[t][:], ACT.Copy, scale=gpos[:, t : t + 1])
            nc.vector.tensor_tensor(page[t][:].indirect(l4[:]), own[t][:], got[t][:], ALU.add)

        fetch_neg(0)
        fetch_neg(1)
        put(0)
        fetch_neg(2)
        put(1)
        put(2)
        fetch_neg(3)
        put(3)
        for t in range(PACK):
            for c, cols in enumerate(chunks):
                src = page[t][:, cols]
                if t == 2 and c < ON_VECTOR:
                    nc.scalar.copy(z2b[c][:, :, 2:4], src.unsqueeze(2).to_broadcast([P, WIDTHS[c], 2]))
                elif t == 3 and c < ON_VECTOR:
                    nc.vector.tensor_copy(z2b[c][:, :, t], src)
                else:
                    nc.scalar.copy(z2b[c][:, :, t], src)

        out_rows = out_0.rearrange("(p t) w -> p t w", t=PACK)
        out_words = out_1[0].rearrange("p c r -> p (c r)").bitcast(I32)
        o_sc = sb("o_sc", [P, U], U8)
        o_w = sb("o_w", [P, U], I32)
        outs = []
        accs = []

        def product(c):
            w = WIDTHS[c]
            qw = sb("qw%d" % c, [P, w], I32, after="res0" if c == 3 else None)
            qs = sb("qs%d" % c, [P, w], U8, after="z2b3" if c == 4 else None)
            nc.vector.quantize_mx(out=qw[:].bitcast(FP8X4), scales=qs[:], in_=z2b[c][:].rearrange("p c t -> p (c t)"))
            per_bank = 512 // w
            banks = []
            for k in range(PACK // per_bank):
                acc = psum.tile([P, per_bank, w], F32, name="bank")
                for e in range(per_bank):
                    t = per_bank * k + e
                    nc.tensor.matmul_mx(
                        out=acc[:, e, :], lhsT=w2w[:, 2 * P * t : 2 * P * (t + 1)].bitcast(FP4X4), lhsT_scale=w2s[:, P * t : P * (t + 1)],
                        rhs=qw[:].bitcast(FP8X4), rhs_scale=qs[:], start=True, stop=True,
                    )
                banks.append(acc)
            accs.append(banks)

        def add_res(c):
            per_bank = 512 // WIDTHS[c]
            o = sb("o%d" % c, [P, PACK, WIDTHS[c]], F32)[:]
            for k, acc in enumerate(accs[c]):
                rows = slice(per_bank * k, per_bank * (k + 1))
                nc.vector.tensor_tensor(o[:, rows, :], acc[:], res_sb[c][:, rows, :], ALU.add)
            nc.sync.dma_start(out_rows[:, :, chunks[c]], o)
            outs.append(o)

        def finish(c):
            ob = sb("ob%d" % c, [P, WIDTHS[c], PACK], BF16)
            interleave(ob[:], outs[c])
            nc.vector.quantize_mx(out=o_w[:, chunks[c]].bitcast(FP8X4), scales=o_sc[:, chunks[c]], in_=ob[:].rearrange("p c t -> p (c t)"))
            if c == 2:
                nc.sync.dma_start(out_words[:, : STARTS[3]], o_w[:, : STARTS[3]])
            elif c == 4:
                nc.sync.dma_start(out_words[:, STARTS[3] :], o_w[:, STARTS[3] :])

        for c in range(3):
            product(c)
        add_res(0)
        product(3)
        product(4)
        add_res(1)
        finish(0)
        add_res(2)
        finish(1)
        add_res(3)
        add_res(4)
        for c in range(2, 5):
            finish(c)
        for q in range(4):
            queue = nc.sync if q % 2 else nc.scalar
            queue.dma_start(out_2[0, 4 * q : 4 * q + 4, :].bitcast(I32), o_sc[32 * q : 32 * q + 4, :].bitcast(I32))
